import numpy as np
import ml_dtypes


def mxq(x, axis, fmt="e4m3"):
    dtype, down = {"e4m3": (ml_dtypes.float8_e4m3fn, 7), "e5m2": (ml_dtypes.float8_e5m2, 14)}[fmt]
    v = np.moveaxis(np.asarray(x, np.float32).astype(ml_dtypes.bfloat16).astype(np.float64), axis, -1)
    blocks = v.reshape(v.shape[:-1] + (-1, 32))
    amax = np.abs(blocks).max(-1, keepdims=True)
    byte = np.maximum(np.where(amax > 0, np.frexp(amax)[1] - 1 + 127, 0) - down, 1)
    scale = np.exp2(byte - 127.0)
    codes = (blocks / scale).astype(np.float32).astype(dtype).astype(np.float64)
    return np.moveaxis((codes * scale).reshape(v.shape), -1, axis)


WIDE = False


def mx_kscale(k):
    if not WIDE:
        return np.ones(k)
    levels = np.array([10, -10, 5, -5, 0])
    if k % 512:
        return np.exp2(np.random.permutation(np.resize(levels, k // 32))).repeat(32)
    a = np.empty((k // 512, 16))
    for p in range(k // 512):
        a[p, :8] = np.random.permutation(np.resize(levels, 8))
        for g in range(8):
            far = levels[np.abs(levels - a[p, g]) >= 10]
            a[p, g + 8] = far[np.random.randint(len(far))]
    return np.exp2(a.ravel()).repeat(32)


def f64(x):
    return np.asarray(x).astype(np.float64)


def striped(idx):
    return np.tile(idx.reshape(-1, 16).T, (8, 1)).astype(np.uint16)


def unstriped(offs):
    return offs[:16].T.reshape(-1).astype(np.int64)


def relu(v):
    return np.maximum(v, 0.0)


K, T, E, C, N = 1024, 1024, 2, 256, 512
M = 512


def by_expert(wq, xq):
    return np.concatenate([wq[e].T @ xq[:, e * C:(e + 1) * C] for e in range(E)], axis=1)


def setup_inputs():
    n = np.random.standard_normal
    s = mx_kscale(K)[:, None]
    v = mx_kscale(N)
    return {
        "xT": (n((K, T)) * s).astype(np.float32),
        "w": (n((E, K, N)) / np.sqrt(K) / s[None] * v[None, None, :]).astype(np.float32),
        "b": (0.3 * n((N, E)) * v[:, None]).astype(np.float32),
        "wp": (n((N, M)) / np.sqrt(N) / v[:, None]).astype(np.float32),
        "gate": np.tile(np.random.uniform(0.2, 1.0, E * C), (N, 1)).astype(np.float32),
        "offs": striped(np.random.permutation(T)[:E * C]),
    }


def reference(xT, w, b, wp, gate, offs):
    idx = unstriped(offs)
    xq = mxq(f64(xT)[:, idx], 0, "e4m3")
    y = by_expert(mxq(f64(w), 1, "e4m3"), xq)
    y = relu(y + np.repeat(f64(b), C, axis=1))
    c = np.zeros((N, T))
    c[:, idx] = f64(gate) * y
    return mxq(f64(wp), 0, "e4m3").T @ mxq(c, 0, "e4m3")

@@ -1,0 +1,248 @@
+from contextlib import ExitStack
+
+import concourse.mybir as mybir
+
+K, T, E, C, N, M = 1024, 1024, 2, 256, 512, 512
+S = E * C
+FLOPS = 2 * K * N * S + 2 * N * M * S
+
+F32 = mybir.dt.float32
+BF16 = mybir.dt.bfloat16
+U32 = mybir.dt.uint32
+I32 = mybir.dt.int32
+U16 = mybir.dt.uint16
+U8 = mybir.dt.uint8
+FP8X4 = mybir.dt.float8_e4m3fn_x4
+RELU = mybir.ActivationFunctionType.Relu
+MULT = mybir.AluOpType.mult
+ADD = mybir.AluOpType.add
+
+P = 128
+J = 4
+KP = P * J
+PASSES = K // KP
+G = 4
+H = T // 2
+
+
+def tile_moe_nxt_lin_relu_kernel(tc, xT, w, b, wp, gate, offs, out):
+    nc = tc.nc
+    with ExitStack() as ctx:
+        keep = ctx.enter_context(tc.tile_pool(name="keep", bufs=1))
+        psum = ctx.enter_context(tc.psum_pool(name="psum", bufs=1))
+
+        offsets = keep.tile([P, S // 16], U16, name="offsets")
+        nc.sync.dma_start(offsets[:], offs)
+        bias = keep.tile([P, G * E], F32, name="bias")
+        nc.sync.dma_start(bias[:], b.rearrange("(p t) e -> p (t e)", t=G))
+
+        xraw = [keep.tile([P, J, T], F32, name=f"xraw{a}") for a in range(PASSES)]
+        wraw = [[keep.tile([P, J, N], F32, name=f"wraw{e}{a}") for a in range(PASSES)] for e in range(E)]
+        wpraw = keep.tile([P, J, M], F32, name="wpraw")
+        gates = keep.tile([P, S], F32, name="gates")
+
+        def load_w(e, a, c0, c1):
+            src = w[e, a * KP : (a + 1) * KP, c0:c1]
+            nc.sync.dma_start(wraw[e][a][:, :, c0:c1], src.rearrange("(p j) n -> p j n", j=J))
+
+        def load_x(a, t0, t1):
+            src = xT[a * KP : (a + 1) * KP, t0:t1]
+            nc.sync.dma_start(xraw[a][:, :, t0:t1], src.rearrange("(p j) t -> p j t", j=J))
+
+        def load_wp(c0, c1):
+            nc.sync.dma_start(wpraw[:, :, c0:c1], wp[:, c0:c1].rearrange("(p j) f -> p j f", j=J))
+
+        load_x(0, 0, 512)
+        load_x(0, 512, 1024)
+        load_w(0, 0, 0, N)
+        load_x(1, 0, 512)
+        load_x(1, 512, 768)
+        load_x(1, 768, 1024)
+        load_w(0, 1, 0, 256)
+        load_w(0, 1, 256, 512)
+        nc.sync.dma_start(gates[:, 0:C], gate[0:P, 0:C])
+        load_wp(0, 256)
+        load_w(1, 0, 0, N)
+        load_w(1, 1, 0, N)
+        nc.sync.dma_start(gates[:, C:S], gate[0:P, C:S])
+        load_wp(256, 512)
+
+        warm = keep.tile([P, 8], F32, name="warm")
+        warmed = keep.tile([P, 8], F32, name="warmed")
+        nc.vector.memset(warm[:], 0.0)
+        nc.scalar.activation(warmed[:], warm[:], RELU)
+
+        xbytes = [keep.tile([P, T], U8, name=f"xbytes{a}", align_bytes=64) for a in range(PASSES)]
+        for a in range(PASSES):
+            nc.vector.memset(xbytes[a][:].bitcast(I32), 0)
+        outt = [keep.tile([P, T], F32, name=f"outt{g}", align_bytes=64) for g in range(G)]
+        for g in range(G):
+            (nc.vector if g % 2 else nc.gpsimd).memset(outt[g][:], 0.0)
+
+        xgrouped = [keep.tile([P, T, J], BF16, name=f"xgrouped{a}", align_bytes=64) for a in range(PASSES)]
+        xcodes = [keep.tile([P, T], U32, name=f"xcodes{a}", align_bytes=64) for a in range(PASSES)]
+        gcodes = [keep.tile([P, S], U32, name=f"gcodes{a}", align_bytes=64) for a in range(PASSES)]
+        gbytes = [keep.tile([P, S], U8, name=f"gbytes{a}", align_bytes=64) for a in range(PASSES)]
+        wgrouped = [[keep.tile([P, G, P, J], BF16, name=f"wgrouped{e}{a}", align_bytes=64) for a in range(PASSES)] for e in range(E)]
+        wcodes = [[keep.tile([P, N], U32, name=f"wcodes{e}{a}", align_bytes=64) for a in range(PASSES)] for e in range(E)]
+        wbytes = [[keep.tile([P, N], U8, name=f"wbytes{e}{a}", align_bytes=64) for a in range(PASSES)] for e in range(E)]
+        wpgrouped = keep.tile([P, M, J], BF16, name="wpgrouped", align_bytes=64)
+        wpcodes = keep.tile([P, M], U32, name="wpcodes", align_bytes=64)
+        wpbytes = keep.tile([P, M], U8, name="wpbytes", align_bytes=64)
+        y = [keep.tile([P, G, C], F32, name=f"y{e}") for e in range(E)]
+        c = [keep.tile([P, C, J], BF16, name=f"c{e}", align_bytes=64) for e in range(E)]
+        ccodes = keep.tile([P, S], U32, name="ccodes", align_bytes=64)
+        cbytes = keep.tile([P, S], U8, name="cbytes", align_bytes=64)
+        oslots = [keep.tile([P, S], F32, name=f"oslots{g}") for g in range(G)]
+        ybank = [psum.tile([P, C], F32, name=f"ybank{t}") for t in range(G)]
+        obank = [psum.tile([P, S], F32, name=f"obank{g}") for g in range(G)]
+
+        def move(engine, dst, src):
+            if engine == "v":
+                nc.vector.tensor_copy(out=dst, in_=src)
+            elif engine == "s":
+                nc.scalar.copy(out=dst, in_=src)
+            else:
+                nc.gpsimd.tensor_scalar(dst, src, 1.0, 0.0, MULT, ADD)
+
+        def group_x(engine, a, t0, t1):
+            move(engine, xgrouped[a][:, t0:t1, :], xraw[a][:, :, t0:t1].rearrange("p j t -> p t j"))
+
+        def group_w(engine, e, a, m0, m1):
+            move(
+                engine,
+                wgrouped[e][a][:, :, m0:m1, :].rearrange("p t m j -> p m t j"),
+                wraw[e][a][:, :, G * m0 : G * m1].rearrange("p j (m t) -> p m t j", t=G),
+            )
+
+        def group_wp(engine, f0, f1):
+            move(engine, wpgrouped[:, f0:f1, :], wpraw[:, :, f0:f1].rearrange("p j f -> p f j"))
+
+        def quantize_x(a, t0, t1):
+            nc.vector.quantize_mx(
+                out=xcodes[a][:, t0:t1].bitcast(FP8X4),
+                scales=xbytes[a][:, t0:t1],
+                in_=xgrouped[a][:, t0:t1, :].rearrange("p t j -> p (t j)"),
+            )
+
+        def quantize_w(e, a, t0, t1):
+            nc.vector.quantize_mx(
+                out=wcodes[e][a][:, t0 * P : t1 * P].bitcast(FP8X4),
+                scales=wbytes[e][a][:, t0 * P : t1 * P],
+                in_=wgrouped[e][a][:, t0:t1, :, :].rearrange("p t m j -> p (t m j)"),
+            )
+
+        def quantize_wp(f0, f1):
+            nc.vector.quantize_mx(
+                out=wpcodes[:, f0:f1].bitcast(FP8X4),
+                scales=wpbytes[:, f0:f1],
+                in_=wpgrouped[:, f0:f1, :].rearrange("p f j -> p (f j)"),
+            )
+
+        def gather(a, s0, s1):
+            columns = offsets[:, s0 // 16 : s1 // 16]
+            nc.vector.tensor_copy(gcodes[a][:, s0:s1], xcodes[a][:].indirect(columns))
+            nc.vector.tensor_copy(gbytes[a][:, s0:s1], xbytes[a][:].indirect(columns))
+
+        def multiply(e, a, t):
+            nc.tensor.matmul_mx(
+                out=ybank[t][:],
+                lhsT=wcodes[e][a][:, t * P : (t + 1) * P].bitcast(FP8X4),
+                lhsT_scale=wbytes[e][a][:, t * P : (t + 1) * P],
+                rhs=gcodes[a][:, e * C : (e + 1) * C].bitcast(FP8X4),
+                rhs_scale=gbytes[a][:, e * C : (e + 1) * C],
+                start=(a == 0),
+                stop=(a == PASSES - 1),
+            )
+
+        def relu(e, t):
+            nc.scalar.activation(y[e][:, t, :], ybank[t][:], RELU, bias=bias[:, t * E + e : t * E + e + 1])
+
+        def apply_gate(engine, e):
+            engine.tensor_tensor(
+                out=c[e][:],
+                in0=y[e][:].rearrange("p t s -> p s t"),
+                in1=gates[:, e * C : (e + 1) * C].unsqueeze(2).to_broadcast([P, C, J]),
+                op=MULT,
+            )
+
+        def quantize_c(e):
+            nc.vector.quantize_mx(
+                out=ccodes[:, e * C : (e + 1) * C].bitcast(FP8X4),
+                scales=cbytes[:, e * C : (e + 1) * C],
+                in_=c[e][:].rearrange("p s j -> p (s j)"),
+            )
+
+        def project(g, s0, s1):
+            nc.tensor.matmul_mx(
+                out=obank[g][:, s0:s1],
+                lhsT=wpcodes[:, g * P : (g + 1) * P].bitcast(FP8X4),
+                lhsT_scale=wpbytes[:, g * P : (g + 1) * P],
+                rhs=ccodes[:, s0:s1].bitcast(FP8X4),
+                rhs_scale=cbytes[:, s0:s1],
+                start=True,
+                stop=True,
+            )
+            nc.scalar.copy(out=oslots[g][:, s0:s1], in_=obank[g][:, s0:s1])
+
+        def scatter(g, s0, s1):
+            nc.vector.tensor_copy(outt[g][:].indirect(offsets[:, s0 // 16 : s1 // 16]), oslots[g][:, s0:s1])
+
+        for t0, t1, cut in ((0, 512, 256), (512, 1024, 768)):
+            group_x("v", 0, t0, cut)
+            group_x("s", 0, cut, t1)
+            quantize_x(0, t0, t1)
+        gather(0, 0, S)
+        group_w("s", 0, 0, 0, 64)
+        group_w("g", 0, 0, 64, 96)
+        group_w("g", 0, 0, 96, 128)
+        quantize_w(0, 0, 0, 4)
+        for t in range(G):
+            multiply(0, 0, t)
+        for t0, t1, cut in ((0, 512, 256), (512, 768, 640), (768, 1024, 928)):
+            group_x("v", 1, t0, cut)
+            group_x("s", 1, cut, t1)
+            quantize_x(1, t0, t1)
+        gather(1, 0, C)
+        group_w("s", 0, 1, 0, 32)
+        group_w("g", 0, 1, 32, 64)
+        group_w("v", 0, 1, 64, 96)
+        group_w("s", 0, 1, 96, 112)
+        group_w("g", 0, 1, 112, 128)
+        for t in (0, 2):
+            quantize_w(0, 1, t, t + 2)
+            for u in (t, t + 1):
+                multiply(0, 1, u)
+                relu(0, u)
+        apply_gate(nc.vector, 0)
+        quantize_c(0)
+        group_wp("s", 0, 128)
+        group_wp("g", 128, 256)
+        quantize_wp(0, 256)
+        for g in range(2):
+            project(g, 0, C)
+        gather(1, C, S)
+        for g in range(2):
+            scatter(g, 0, C)
+
+        for a in range(PASSES):
+            group_w("s", 1, a, 0, 64)
+            group_w("g", 1, a, 64, 96)
+            group_w("g", 1, a, 96, 128)
+            quantize_w(1, a, 0, 4)
+            for t in range(G):
+                multiply(1, a, t)
+                if a == PASSES - 1:
+                    relu(1, t)
+        apply_gate(nc.vector, 1)
+        quantize_c(1)
+        group_wp("s", 256, 384)
+        group_wp("g", 384, 512)
+        quantize_wp(256, 512)
+        for g in range(G):
+            s0 = C if g < 2 else 0
+            project(g, s0, S)
+        for g in range(G):
+            s0 = C if g < 2 else 0
+            scatter(g, s0, S)
+            nc.sync.dma_start(out[g * P : (g + 1) * P, :], outt[g][:])

@@ -32,9 +32,7 @@ def tile_moe_nxt_lin_relu_kernel(tc, xT, w, b, wp, gate, offs, out):
         psum = ctx.enter_context(tc.psum_pool(name="psum", bufs=1))
 
         offsets = keep.tile([P, S // 16], U16, name="offsets")
-        nc.sync.dma_start(offsets[:], offs)
         bias = keep.tile([P, G * E], F32, name="bias")
-        nc.sync.dma_start(bias[:], b.rearrange("(p t) e -> p (t e)", t=G))
 
         xraw = [keep.tile([P, J, T], F32, name=f"xraw{a}") for a in range(PASSES)]
         wraw = [[keep.tile([P, J, N], F32, name=f"wraw{e}{a}") for a in range(PASSES)] for e in range(E)]
@@ -52,37 +50,39 @@ def tile_moe_nxt_lin_relu_kernel(tc, xT, w, b, wp, gate, offs, out):
         def load_wp(c0, c1):
             nc.sync.dma_start(wpraw[:, :, c0:c1], wp[:, c0:c1].rearrange("(p j) f -> p j f", j=J))
 
-        load_x(0, 0, 512)
-        load_x(0, 512, 1024)
-        load_w(0, 0, 0, N)
-        load_x(1, 0, 512)
-        load_x(1, 512, 768)
+        load_x(0, 0, 256)
+        nc.sync.dma_start(offsets[:], offs)
+        nc.sync.dma_start(bias[:], b.rearrange("(p t) e -> p (t e)", t=G))
+        load_x(1, 0, 256)
+        load_x(0, 256, 768)
+        load_x(1, 256, 768)
+        load_x(0, 768, 1024)
         load_x(1, 768, 1024)
+        load_w(0, 0, 0, 512)
         load_w(0, 1, 0, 256)
         load_w(0, 1, 256, 512)
-        nc.sync.dma_start(gates[:, 0:C], gate[0:P, 0:C])
+        load_w(1, 0, 0, 512)
         load_wp(0, 256)
-        load_w(1, 0, 0, N)
-        load_w(1, 1, 0, N)
-        nc.sync.dma_start(gates[:, C:S], gate[0:P, C:S])
+        nc.sync.dma_start(gates[:, 0:C], gate[0:P, 0:C])
+        load_w(1, 1, 0, 512)
         load_wp(256, 512)
+        nc.sync.dma_start(gates[:, C:S], gate[0:P, C:S])
 
         warm = keep.tile([P, 8], F32, name="warm")
         warmed = keep.tile([P, 8], F32, name="warmed")
         nc.vector.memset(warm[:], 0.0)
         nc.scalar.activation(warmed[:], warm[:], RELU)
 
-        xbytes = [keep.tile([P, T], U8, name=f"xbytes{a}", align_bytes=64) for a in range(PASSES)]
-        for a in range(PASSES):
-            nc.vector.memset(xbytes[a][:].bitcast(I32), 0)
+        xbytes = keep.tile([P, T], U8, name="xbytes", align_bytes=64)
+        nc.vector.memset(xbytes[:].bitcast(I32), 0)
         outt = [keep.tile([P, T], F32, name=f"outt{g}", align_bytes=64) for g in range(G)]
         for g in range(G):
-            (nc.vector if g % 2 else nc.gpsimd).memset(outt[g][:], 0.0)
+            nc.gpsimd.memset(outt[g][:], 0.0)
 
         xgrouped = [keep.tile([P, T, J], BF16, name=f"xgrouped{a}", align_bytes=64) for a in range(PASSES)]
         xcodes = [keep.tile([P, T], U32, name=f"xcodes{a}", align_bytes=64) for a in range(PASSES)]
         gcodes = [keep.tile([P, S], U32, name=f"gcodes{a}", align_bytes=64) for a in range(PASSES)]
-        gbytes = [keep.tile([P, S], U8, name=f"gbytes{a}", align_bytes=64) for a in range(PASSES)]
+        gbytes = keep.tile([P, S], U8, name="gbytes", align_bytes=64)
         wgrouped = [[keep.tile([P, G, P, J], BF16, name=f"wgrouped{e}{a}", align_bytes=64) for a in range(PASSES)] for e in range(E)]
         wcodes = [[keep.tile([P, N], U32, name=f"wcodes{e}{a}", align_bytes=64) for a in range(PASSES)] for e in range(E)]
         wbytes = [[keep.tile([P, N], U8, name=f"wbytes{e}{a}", align_bytes=64) for a in range(PASSES)] for e in range(E)]
@@ -106,22 +106,34 @@ def tile_moe_nxt_lin_relu_kernel(tc, xT, w, b, wp, gate, offs, out):
                 nc.gpsimd.tensor_scalar(dst, src, 1.0, 0.0, MULT, ADD)
 
         def group_x(engine, a, t0, t1):
-            move(engine, xgrouped[a][:, t0:t1, :], xraw[a][:, :, t0:t1].rearrange("p j t -> p t j"))
-
-        def group_w(engine, e, a, m0, m1):
             move(
                 engine,
-                wgrouped[e][a][:, :, m0:m1, :].rearrange("p t m j -> p m t j"),
-                wraw[e][a][:, :, G * m0 : G * m1].rearrange("p j (m t) -> p m t j", t=G),
+                xgrouped[a][:, t0:t1, :].rearrange("p (c i) j -> p c j i", i=4),
+                xraw[a][:, :, t0:t1].rearrange("p j (c i) -> p c j i", i=4),
+            )
+
+        def group_w(engine, e, a, m0, m1):
+            order = "p m t j" if engine == "g" else "p m j t"
+            move(
+                engine,
+                wgrouped[e][a][:, :, m0:m1, :].rearrange("p t m j -> " + order),
+                wraw[e][a][:, :, G * m0 : G * m1].rearrange("p j (m t) -> " + order, t=G),
             )
 
         def group_wp(engine, f0, f1):
-            move(engine, wpgrouped[:, f0:f1, :], wpraw[:, :, f0:f1].rearrange("p j f -> p f j"))
+            if engine == "g":
+                move(engine, wpgrouped[:, f0:f1, :], wpraw[:, :, f0:f1].rearrange("p j f -> p f j"))
+            else:
+                move(
+                    engine,
+                    wpgrouped[:, f0:f1, :].rearrange("p (c i) j -> p c j i", i=4),
+                    wpraw[:, :, f0:f1].rearrange("p j (c i) -> p c j i", i=4),
+                )
 
         def quantize_x(a, t0, t1):
             nc.vector.quantize_mx(
                 out=xcodes[a][:, t0:t1].bitcast(FP8X4),
-                scales=xbytes[a][:, t0:t1],
+                scales=xbytes[4 * a :, t0:t1],
                 in_=xgrouped[a][:, t0:t1, :].rearrange("p t j -> p (t j)"),
             )
 
@@ -139,10 +151,11 @@ def tile_moe_nxt_lin_relu_kernel(tc, xT, w, b, wp, gate, offs, out):
                 in_=wpgrouped[:, f0:f1, :].rearrange("p f j -> p (f j)"),
             )
 
-        def gather(a, s0, s1):
-            columns = offsets[:, s0 // 16 : s1 // 16]
-            nc.vector.tensor_copy(gcodes[a][:, s0:s1], xcodes[a][:].indirect(columns))
-            nc.vector.tensor_copy(gbytes[a][:, s0:s1], xbytes[a][:].indirect(columns))
+        def gather_words(a, s0, s1):
+            nc.vector.tensor_copy(gcodes[a][:, s0:s1], xcodes[a][:].indirect(offsets[:, s0 // 16 : s1 // 16]))
+
+        def gather_bytes(s0, s1):
+            nc.vector.tensor_copy(gbytes[:, s0:s1], xbytes[:].indirect(offsets[:, s0 // 16 : s1 // 16]))
 
         def multiply(e, a, t):
             nc.tensor.matmul_mx(
@@ -150,7 +163,7 @@ def tile_moe_nxt_lin_relu_kernel(tc, xT, w, b, wp, gate, offs, out):
                 lhsT=wcodes[e][a][:, t * P : (t + 1) * P].bitcast(FP8X4),
                 lhsT_scale=wbytes[e][a][:, t * P : (t + 1) * P],
                 rhs=gcodes[a][:, e * C : (e + 1) * C].bitcast(FP8X4),
-                rhs_scale=gbytes[a][:, e * C : (e + 1) * C],
+                rhs_scale=gbytes[4 * a :, e * C : (e + 1) * C],
                 start=(a == 0),
                 stop=(a == PASSES - 1),
             )
@@ -188,27 +201,31 @@ def tile_moe_nxt_lin_relu_kernel(tc, xT, w, b, wp, gate, offs, out):
         def scatter(g, s0, s1):
             nc.vector.tensor_copy(outt[g][:].indirect(offsets[:, s0 // 16 : s1 // 16]), oslots[g][:, s0:s1])
 
-        for t0, t1, cut in ((0, 512, 256), (512, 1024, 768)):
-            group_x("v", 0, t0, cut)
-            group_x("s", 0, cut, t1)
-            quantize_x(0, t0, t1)
-        gather(0, 0, S)
-        group_w("s", 0, 0, 0, 64)
-        group_w("g", 0, 0, 64, 96)
-        group_w("g", 0, 0, 96, 128)
+        def x_chunk(a, t0, t1, cut):
+            if cut > t0:
+                group_x("v", a, t0, cut)
+            if cut < t1:
+                group_x("s", a, cut, t1)
+            quantize_x(a, t0, t1)
+
+        x_chunk(0, 0, 256, 256)
+        x_chunk(0, 256, 768, 640)
+        x_chunk(0, 768, 1024, 768)
+        gather_words(0, 0, S)
+        group_w("g", 0, 0, 0, 56)
+        group_w("s", 0, 0, 56, 128)
         quantize_w(0, 0, 0, 4)
+        x_chunk(1, 0, 256, 0)
+        x_chunk(1, 256, 768, 576)
+        x_chunk(1, 768, 1024, 960)
+        gather_bytes(0, C)
+        gather_words(1, 0, C)
         for t in range(G):
             multiply(0, 0, t)
-        for t0, t1, cut in ((0, 512, 256), (512, 768, 640), (768, 1024, 928)):
-            group_x("v", 1, t0, cut)
-            group_x("s", 1, cut, t1)
-            quantize_x(1, t0, t1)
-        gather(1, 0, C)
-        group_w("s", 0, 1, 0, 32)
-        group_w("g", 0, 1, 32, 64)
-        group_w("v", 0, 1, 64, 96)
-        group_w("s", 0, 1, 96, 112)
-        group_w("g", 0, 1, 112, 128)
+        group_w("g", 0, 1, 0, 32)
+        group_w("s", 0, 1, 32, 64)
+        group_w("v", 0, 1, 64, 80)
+        group_w("s", 0, 1, 80, 128)
         for t in (0, 2):
             quantize_w(0, 1, t, t + 2)
             for u in (t, t + 1):
@@ -216,33 +233,35 @@ def tile_moe_nxt_lin_relu_kernel(tc, xT, w, b, wp, gate, offs, out):
                 relu(0, u)
         apply_gate(nc.vector, 0)
         quantize_c(0)
-        group_wp("s", 0, 128)
-        group_wp("g", 128, 256)
+        group_wp("v", 0, 32)
+        group_wp("s", 32, 256)
         quantize_wp(0, 256)
-        for g in range(2):
-            project(g, 0, C)
-        gather(1, C, S)
-        for g in range(2):
-            scatter(g, 0, C)
-
-        for a in range(PASSES):
-            group_w("s", 1, a, 0, 64)
-            group_w("g", 1, a, 64, 96)
-            group_w("g", 1, a, 96, 128)
-            quantize_w(1, a, 0, 4)
-            for t in range(G):
-                multiply(1, a, t)
-                if a == PASSES - 1:
-                    relu(1, t)
-        apply_gate(nc.vector, 1)
-        quantize_c(1)
-        group_wp("s", 256, 384)
-        group_wp("g", 384, 512)
+        group_wp("v", 256, 320)
+        group_wp("s", 320, 512)
         quantize_wp(256, 512)
         for g in range(G):
-            s0 = C if g < 2 else 0
-            project(g, s0, S)
+            project(g, 0, C)
+        gather_words(1, C, S)
+        gather_bytes(C, S)
+        group_w("v", 1, 0, 0, 112)
+        group_w("s", 1, 0, 112, 128)
+        quantize_w(1, 0, 0, 4)
+        for t in range(G):
+            multiply(1, 0, t)
+        scatter(1, 0, C)
+        scatter(0, 0, C)
+        group_w("v", 1, 1, 0, 72)
+        group_w("s", 1, 1, 72, 128)
+        quantize_w(1, 1, 0, 4)
+        for t in range(G):
+            multiply(1, 1, t)
+            relu(1, t)
+        scatter(2, 0, C)
+        apply_gate(nc.gpsimd, 1)
+        quantize_c(1)
+        scatter(3, 0, C)
         for g in range(G):
-            s0 = C if g < 2 else 0
-            scatter(g, s0, S)
+            project(g, C, S)
+        for g in range(G):
+            scatter(g, C, S)
             nc.sync.dma_start(out[g * P : (g + 1) * P, :], outt[g][:])

@@ -34,39 +34,36 @@ def tile_moe_nxt_lin_relu_kernel(tc, xT, w, b, wp, gate, offs, out):
         offsets = keep.tile([P, S // 16], U16, name="offsets")
         bias = keep.tile([P, G * E], F32, name="bias")
 
-        xraw = [keep.tile([P, J, T], F32, name=f"xraw{a}") for a in range(PASSES)]
-        wraw = [[keep.tile([P, J, N], F32, name=f"wraw{e}{a}") for a in range(PASSES)] for e in range(E)]
-        wpraw = keep.tile([P, J, M], F32, name="wpraw")
-        gates = keep.tile([P, S], F32, name="gates")
-
-        def load_w(e, a, c0, c1):
-            src = w[e, a * KP : (a + 1) * KP, c0:c1]
-            nc.sync.dma_start(wraw[e][a][:, :, c0:c1], src.rearrange("(p j) n -> p j n", j=J))
-
-        def load_x(a, t0, t1):
+        x_chunks = [(1, 0, 512, 384), (0, 0, 256, 0), (0, 256, 768, 224), (1, 512, 768, 192), (1, 768, 1024, 256), (0, 768, 1024, 96)]
+        xraw = {}
+        for k, (a, t0, t1, cut) in enumerate(x_chunks):
+            xraw[a, t0] = keep.tile([P, J, t1 - t0], F32, name=f"xraw{a}{t0}")
             src = xT[a * KP : (a + 1) * KP, t0:t1]
-            nc.sync.dma_start(xraw[a][:, :, t0:t1], src.rearrange("(p j) t -> p j t", j=J))
+            nc.sync.dma_start(xraw[a, t0][:], src.rearrange("(p j) t -> p j t", j=J))
+            if k == 0:
+                nc.sync.dma_start(offsets[:], offs)
+                nc.sync.dma_start(bias[:], b.rearrange("(p t) e -> p (t e)", t=G))
+        wraw = [[keep.tile([P, J, N], F32, name=f"wraw{e}{a}") for a in range(PASSES)] for e in range(E)]
+        wpraw = [keep.tile([P, J, M // 2], F32, name=f"wpraw{h}") for h in range(2)]
+        gates = [keep.tile([P, C], F32, name=f"gates{e}") for e in range(E)]
 
-        def load_wp(c0, c1):
-            nc.sync.dma_start(wpraw[:, :, c0:c1], wp[:, c0:c1].rearrange("(p j) f -> p j f", j=J))
+        def load_w(e, a):
+            nc.sync.dma_start(wraw[e][a][:], w[e, a * KP : (a + 1) * KP, :].rearrange("(p j) n -> p j n", j=J))
 
-        load_x(0, 0, 256)
-        nc.sync.dma_start(offsets[:], offs)
-        nc.sync.dma_start(bias[:], b.rearrange("(p t) e -> p (t e)", t=G))
-        load_x(1, 0, 256)
-        load_x(0, 256, 768)
-        load_x(1, 256, 768)
-        load_x(0, 768, 1024)
-        load_x(1, 768, 1024)
-        load_w(0, 0, 0, 512)
-        load_w(0, 1, 0, 256)
-        load_w(0, 1, 256, 512)
-        load_w(1, 0, 0, 512)
-        load_wp(0, 256)
-        nc.sync.dma_start(gates[:, 0:C], gate[0:P, 0:C])
-        load_w(1, 1, 0, 512)
-        load_wp(256, 512)
-        nc.sync.dma_start(gates[:, C:S], gate[0:P, C:S])
+        def load_wp(h):
+            nc.sync.dma_start(wpraw[h][:], wp[:, h * 256 : (h + 1) * 256].rearrange("(p j) f -> p j f", j=J))
+
+        def load_gates(e):
+            nc.sync.dma_start(gates[e][:], gate[0:P, e * C : (e + 1) * C])
+
+        load_w(0, 0)
+        load_w(0, 1)
+        load_wp(0)
+        load_w(1, 0)
+        load_gates(0)
+        load_w(1, 1)
+        load_wp(1)
+        load_gates(1)
 
         warm = keep.tile([P, 8], F32, name="warm")
         warmed = keep.tile([P, 8], F32, name="warmed")
@@ -83,17 +80,22 @@ def tile_moe_nxt_lin_relu_kernel(tc, xT, w, b, wp, gate, offs, out):
         xcodes = [keep.tile([P, T], U32, name=f"xcodes{a}", align_bytes=64) for a in range(PASSES)]
         gcodes = [keep.tile([P, S], U32, name=f"gcodes{a}", align_bytes=64) for a in range(PASSES)]
         gbytes = keep.tile([P, S], U8, name="gbytes", align_bytes=64)
-        wgrouped = [[keep.tile([P, G, P, J], BF16, name=f"wgrouped{e}{a}", align_bytes=64) for a in range(PASSES)] for e in range(E)]
+        wgrouped = [
+            [
+                keep.tile([P, G, P, J], BF16, name=f"wgrouped{e}{a}", tag="late" if e and a else f"wgrouped{e}{a}", align_bytes=64)
+                for a in range(PASSES)
+            ]
+            for e in range(E)
+        ]
         wcodes = [[keep.tile([P, N], U32, name=f"wcodes{e}{a}", align_bytes=64) for a in range(PASSES)] for e in range(E)]
         wbytes = [[keep.tile([P, N], U8, name=f"wbytes{e}{a}", align_bytes=64) for a in range(PASSES)] for e in range(E)]
         wpgrouped = keep.tile([P, M, J], BF16, name="wpgrouped", align_bytes=64)
         wpcodes = keep.tile([P, M], U32, name="wpcodes", align_bytes=64)
         wpbytes = keep.tile([P, M], U8, name="wpbytes", align_bytes=64)
         y = [keep.tile([P, G, C], F32, name=f"y{e}") for e in range(E)]
-        c = [keep.tile([P, C, J], BF16, name=f"c{e}", align_bytes=64) for e in range(E)]
+        c = [keep.tile([P, C, J], BF16, name=f"c{e}", tag=f"c{e}", align_bytes=64) for e in range(E)]
         ccodes = keep.tile([P, S], U32, name="ccodes", align_bytes=64)
         cbytes = keep.tile([P, S], U8, name="cbytes", align_bytes=64)
-        oslots = [keep.tile([P, S], F32, name=f"oslots{g}") for g in range(G)]
         ybank = [psum.tile([P, C], F32, name=f"ybank{t}") for t in range(G)]
         obank = [psum.tile([P, S], F32, name=f"obank{g}") for g in range(G)]
 
@@ -105,30 +107,29 @@ def tile_moe_nxt_lin_relu_kernel(tc, xT, w, b, wp, gate, offs, out):
             else:
                 nc.gpsimd.tensor_scalar(dst, src, 1.0, 0.0, MULT, ADD)
 
-        def group_x(engine, a, t0, t1):
+        def group_x(engine, a, t0, lo, hi):
             move(
                 engine,
-                xgrouped[a][:, t0:t1, :].rearrange("p (c i) j -> p c j i", i=4),
-                xraw[a][:, :, t0:t1].rearrange("p j (c i) -> p c j i", i=4),
+                xgrouped[a][:, t0 + lo : t0 + hi, :].rearrange("p (c i) j -> p c j i", i=4),
+                xraw[a, t0][:, :, lo:hi].rearrange("p j (c i) -> p c j i", i=4),
             )
 
-        def group_w(engine, e, a, m0, m1):
+        def group_w(engine, e, a, lo, hi):
             order = "p m t j" if engine == "g" else "p m j t"
             move(
                 engine,
-                wgrouped[e][a][:, :, m0:m1, :].rearrange("p t m j -> " + order),
-                wraw[e][a][:, :, G * m0 : G * m1].rearrange("p j (m t) -> " + order, t=G),
+                wgrouped[e][a][:, lo:hi, :, :].rearrange("p t m j -> " + order),
+                wraw[e][a][:].rearrange("p j (m t) -> " + order, t=G)[:, :, lo:hi, :]
+                if engine == "g"
+                else wraw[e][a][:].rearrange("p j (m t) -> " + order, t=G)[:, :, :, lo:hi],
             )
 
-        def group_wp(engine, f0, f1):
-            if engine == "g":
-                move(engine, wpgrouped[:, f0:f1, :], wpraw[:, :, f0:f1].rearrange("p j f -> p f j"))
-            else:
-                move(
-                    engine,
-                    wpgrouped[:, f0:f1, :].rearrange("p (c i) j -> p c j i", i=4),
-                    wpraw[:, :, f0:f1].rearrange("p j (c i) -> p c j i", i=4),
-                )
+        def group_wp(engine, h, lo, hi):
+            move(
+                engine,
+                wpgrouped[:, h * 256 + lo : h * 256 + hi, :].rearrange("p (c i) j -> p c j i", i=4),
+                wpraw[h][:, :, lo:hi].rearrange("p j (c i) -> p c j i", i=4),
+            )
 
         def quantize_x(a, t0, t1):
             nc.vector.quantize_mx(
@@ -175,7 +176,7 @@ def tile_moe_nxt_lin_relu_kernel(tc, xT, w, b, wp, gate, offs, out):
             engine.tensor_tensor(
                 out=c[e][:],
                 in0=y[e][:].rearrange("p t s -> p s t"),
-                in1=gates[:, e * C : (e + 1) * C].unsqueeze(2).to_broadcast([P, C, J]),
+                in1=gates[e][:].unsqueeze(2).to_broadcast([P, C, J]),
                 op=MULT,
             )
 
@@ -201,31 +202,23 @@ def tile_moe_nxt_lin_relu_kernel(tc, xT, w, b, wp, gate, offs, out):
         def scatter(g, s0, s1):
             nc.vector.tensor_copy(outt[g][:].indirect(offsets[:, s0 // 16 : s1 // 16]), oslots[g][:, s0:s1])
 
-        def x_chunk(a, t0, t1, cut):
-            if cut > t0:
-                group_x("v", a, t0, cut)
-            if cut < t1:
-                group_x("s", a, cut, t1)
+        for a, t0, t1, cut in x_chunks:
+            if cut > 0:
+                group_x("v", a, t0, 0, cut)
+            if cut < t1 - t0:
+                group_x("s", a, t0, cut, t1 - t0)
             quantize_x(a, t0, t1)
-
-        x_chunk(0, 0, 256, 256)
-        x_chunk(0, 256, 768, 640)
-        x_chunk(0, 768, 1024, 768)
+            if (a, t1) == (1, 1024):
+                gather_words(1, 0, C)
         gather_words(0, 0, S)
-        group_w("g", 0, 0, 0, 56)
-        group_w("s", 0, 0, 56, 128)
+        group_w("g", 0, 0, 0, 2)
+        group_w("s", 0, 0, 2, 4)
         quantize_w(0, 0, 0, 4)
-        x_chunk(1, 0, 256, 0)
-        x_chunk(1, 256, 768, 576)
-        x_chunk(1, 768, 1024, 960)
         gather_bytes(0, C)
-        gather_words(1, 0, C)
         for t in range(G):
             multiply(0, 0, t)
-        group_w("g", 0, 1, 0, 32)
-        group_w("s", 0, 1, 32, 64)
-        group_w("v", 0, 1, 64, 80)
-        group_w("s", 0, 1, 80, 128)
+        group_w("s", 0, 1, 0, 2)
+        group_w("v", 0, 1, 2, 4)
         for t in (0, 2):
             quantize_w(0, 1, t, t + 2)
             for u in (t, t + 1):
@@ -233,32 +226,30 @@ def tile_moe_nxt_lin_relu_kernel(tc, xT, w, b, wp, gate, offs, out):
                 relu(0, u)
         apply_gate(nc.vector, 0)
         quantize_c(0)
-        group_wp("v", 0, 32)
-        group_wp("s", 32, 256)
-        quantize_wp(0, 256)
-        group_wp("v", 256, 320)
-        group_wp("s", 320, 512)
-        quantize_wp(256, 512)
-        for g in range(G):
-            project(g, 0, C)
+        for h, cut in ((0, 32), (1, 64)):
+            group_wp("v", h, 0, cut)
+            group_wp("s", h, cut, 256)
+            quantize_wp(h * 256, h * 256 + 256)
         gather_words(1, C, S)
         gather_bytes(C, S)
-        group_w("v", 1, 0, 0, 112)
-        group_w("s", 1, 0, 112, 128)
-        quantize_w(1, 0, 0, 4)
-        for t in range(G):
-            multiply(1, 0, t)
-        scatter(1, 0, C)
-        scatter(0, 0, C)
-        group_w("v", 1, 1, 0, 72)
-        group_w("s", 1, 1, 72, 128)
-        quantize_w(1, 1, 0, 4)
-        for t in range(G):
-            multiply(1, 1, t)
-            relu(1, t)
-        scatter(2, 0, C)
+        for a in range(PASSES):
+            group_w("s", 1, a, 0, 2)
+            group_w("v", 1, a, 2, 4)
+            quantize_w(1, a, 0, 4)
+            for t in range(G):
+                multiply(1, a, t)
+                if a == PASSES - 1:
+                    relu(1, t)
+        late = keep.tile([P, G - 1, S], F32, name="late", tag="late", align_bytes=64)
+        oslots = [late[:, g, :] for g in range(G - 1)]
+        for g in range(G - 1):
+            project(g, 0, C)
+            scatter(g, 0, C)
         apply_gate(nc.gpsimd, 1)
         quantize_c(1)
+        last = keep.tile([P, S], F32, name="last", tag="c1", align_bytes=64)
+        oslots.append(last[:])
+        project(3, 0, C)
         scatter(3, 0, C)
         for g in range(G):
             project(g, C, S)

@@ -34,7 +34,7 @@ def tile_moe_nxt_lin_relu_kernel(tc, xT, w, b, wp, gate, offs, out):
         offsets = keep.tile([P, S // 16], U16, name="offsets")
         bias = keep.tile([P, G * E], F32, name="bias")
 
-        x_chunks = [(1, 0, 512, 384), (0, 0, 256, 0), (0, 256, 768, 224), (1, 512, 768, 192), (1, 768, 1024, 256), (0, 768, 1024, 96)]
+        x_chunks = [(1, 0, 512, 256), (1, 512, 1024, 256), (0, 0, 512, 128), (0, 512, 1024, 320)]
         xraw = {}
         for k, (a, t0, t1, cut) in enumerate(x_chunks):
             xraw[a, t0] = keep.tile([P, J, t1 - t0], F32, name=f"xraw{a}{t0}")
@@ -79,10 +79,10 @@ def tile_moe_nxt_lin_relu_kernel(tc, xT, w, b, wp, gate, offs, out):
         xgrouped = [keep.tile([P, T, J], BF16, name=f"xgrouped{a}", align_bytes=64) for a in range(PASSES)]
         xcodes = [keep.tile([P, T], U32, name=f"xcodes{a}", align_bytes=64) for a in range(PASSES)]
         gcodes = [keep.tile([P, S], U32, name=f"gcodes{a}", align_bytes=64) for a in range(PASSES)]
-        gbytes = keep.tile([P, S], U8, name="gbytes", align_bytes=64)
+        gbytes = [keep.tile([P, C], U8, name="gbytes0", align_bytes=64)]
         wgrouped = [
             [
-                keep.tile([P, G, P, J], BF16, name=f"wgrouped{e}{a}", tag="late" if e and a else f"wgrouped{e}{a}", align_bytes=64)
+                keep.tile([P, G, P, J], BF16, name=f"wgrouped{e}{a}", tag=f"wgrouped{e}{a}", align_bytes=64)
                 for a in range(PASSES)
             ]
             for e in range(E)
@@ -92,8 +92,8 @@ def tile_moe_nxt_lin_relu_kernel(tc, xT, w, b, wp, gate, offs, out):
         wpgrouped = keep.tile([P, M, J], BF16, name="wpgrouped", align_bytes=64)
         wpcodes = keep.tile([P, M], U32, name="wpcodes", align_bytes=64)
         wpbytes = keep.tile([P, M], U8, name="wpbytes", align_bytes=64)
-        y = [keep.tile([P, G, C], F32, name=f"y{e}") for e in range(E)]
-        c = [keep.tile([P, C, J], BF16, name=f"c{e}", tag=f"c{e}", align_bytes=64) for e in range(E)]
+        y = [keep.tile([P, G, C], F32, name=f"y{e}", tag=f"y{e}", align_bytes=64) for e in range(E)]
+        c = [keep.tile([P, C, J], BF16, name=f"c{e}", align_bytes=64) for e in range(E)]
         ccodes = keep.tile([P, S], U32, name="ccodes", align_bytes=64)
         cbytes = keep.tile([P, S], U8, name="cbytes", align_bytes=64)
         ybank = [psum.tile([P, C], F32, name=f"ybank{t}") for t in range(G)]
@@ -155,8 +155,8 @@ def tile_moe_nxt_lin_relu_kernel(tc, xT, w, b, wp, gate, offs, out):
         def gather_words(a, s0, s1):
             nc.vector.tensor_copy(gcodes[a][:, s0:s1], xcodes[a][:].indirect(offsets[:, s0 // 16 : s1 // 16]))
 
-        def gather_bytes(s0, s1):
-            nc.vector.tensor_copy(gbytes[:, s0:s1], xbytes[:].indirect(offsets[:, s0 // 16 : s1 // 16]))
+        def gather_bytes(e):
+            nc.vector.tensor_copy(gbytes[e][:], xbytes[:].indirect(offsets[:, e * 16 : (e + 1) * 16]))
 
         def multiply(e, a, t):
             nc.tensor.matmul_mx(
@@ -164,7 +164,7 @@ def tile_moe_nxt_lin_relu_kernel(tc, xT, w, b, wp, gate, offs, out):
                 lhsT=wcodes[e][a][:, t * P : (t + 1) * P].bitcast(FP8X4),
                 lhsT_scale=wbytes[e][a][:, t * P : (t + 1) * P],
                 rhs=gcodes[a][:, e * C : (e + 1) * C].bitcast(FP8X4),
-                rhs_scale=gbytes[4 * a :, e * C : (e + 1) * C],
+                rhs_scale=gbytes[e][4 * a :, :],
                 start=(a == 0),
                 stop=(a == PASSES - 1),
             )
@@ -203,23 +203,20 @@ def tile_moe_nxt_lin_relu_kernel(tc, xT, w, b, wp, gate, offs, out):
             nc.vector.tensor_copy(outt[g][:].indirect(offsets[:, s0 // 16 : s1 // 16]), oslots[g][:, s0:s1])
 
         for a, t0, t1, cut in x_chunks:
-            if cut > 0:
-                group_x("v", a, t0, 0, cut)
-            if cut < t1 - t0:
-                group_x("s", a, t0, cut, t1 - t0)
+            group_x("v", a, t0, 0, cut)
+            group_x("s", a, t0, cut, t1 - t0)
             quantize_x(a, t0, t1)
-            if (a, t1) == (1, 1024):
-                gather_words(1, 0, C)
-        gather_words(0, 0, S)
+            if t1 == T:
+                gather_words(a, 0, S)
         group_w("g", 0, 0, 0, 2)
         group_w("s", 0, 0, 2, 4)
         quantize_w(0, 0, 0, 4)
-        gather_bytes(0, C)
+        gather_bytes(0)
         for t in range(G):
             multiply(0, 0, t)
-        group_w("s", 0, 1, 0, 2)
-        group_w("v", 0, 1, 2, 4)
         for t in (0, 2):
+            group_w("s", 0, 1, t, t + 1)
+            group_w("v", 0, 1, t + 1, t + 2)
             quantize_w(0, 1, t, t + 2)
             for u in (t, t + 1):
                 multiply(0, 1, u)
@@ -230,8 +227,8 @@ def tile_moe_nxt_lin_relu_kernel(tc, xT, w, b, wp, gate, offs, out):
             group_wp("v", h, 0, cut)
             group_wp("s", h, cut, 256)
             quantize_wp(h * 256, h * 256 + 256)
-        gather_words(1, C, S)
-        gather_bytes(C, S)
+        gbytes.append(keep.tile([P, C], U8, name="gbytes1", tag="wgrouped01", align_bytes=64))
+        gather_bytes(1)
         for a in range(PASSES):
             group_w("s", 1, a, 0, 2)
             group_w("v", 1, a, 2, 4)
@@ -240,14 +237,14 @@ def tile_moe_nxt_lin_relu_kernel(tc, xT, w, b, wp, gate, offs, out):
                 multiply(1, a, t)
                 if a == PASSES - 1:
                     relu(1, t)
-        late = keep.tile([P, G - 1, S], F32, name="late", tag="late", align_bytes=64)
+        late = keep.tile([P, G - 1, S], F32, name="late", tag="wgrouped11", align_bytes=64)
         oslots = [late[:, g, :] for g in range(G - 1)]
         for g in range(G - 1):
             project(g, 0, C)
             scatter(g, 0, C)
         apply_gate(nc.gpsimd, 1)
         quantize_c(1)
-        last = keep.tile([P, S], F32, name="last", tag="c1", align_bytes=64)
+        last = keep.tile([P, S], F32, name="last", tag="y1", align_bytes=64)
         oslots.append(last[:])
         project(3, 0, C)
         scatter(3, 0, C)

from contextlib import ExitStack

import concourse.mybir as mybir

K, T, E, C, N, M = 1024, 1024, 2, 256, 512, 512
S = E * C
FLOPS = 2 * K * N * S + 2 * N * M * S

F32 = mybir.dt.float32
BF16 = mybir.dt.bfloat16
U32 = mybir.dt.uint32
I32 = mybir.dt.int32
U16 = mybir.dt.uint16
U8 = mybir.dt.uint8
FP8X4 = mybir.dt.float8_e4m3fn_x4
RELU = mybir.ActivationFunctionType.Relu
MULT = mybir.AluOpType.mult
ADD = mybir.AluOpType.add

P = 128
J = 4
KP = P * J
PASSES = K // KP
G = 4
H = T // 2


def tile_moe_nxt_lin_relu_kernel(tc, xT, w, b, wp, gate, offs, out):
    nc = tc.nc
    with ExitStack() as ctx:
        keep = ctx.enter_context(tc.tile_pool(name="keep", bufs=1))
        psum = ctx.enter_context(tc.psum_pool(name="psum", bufs=1))

        offsets = keep.tile([P, S // 16], U16, name="offsets")
        bias = keep.tile([P, G * E], F32, name="bias")

        x_chunks = [(1, 0, 512, 256), (1, 512, 1024, 256), (0, 0, 512, 128), (0, 512, 1024, 320)]
        xraw = {}
        for k, (a, t0, t1, cut) in enumerate(x_chunks):
            xraw[a, t0] = keep.tile([P, J, t1 - t0], F32, name=f"xraw{a}{t0}")
            src = xT[a * KP : (a + 1) * KP, t0:t1]
            nc.sync.dma_start(xraw[a, t0][:], src.rearrange("(p j) t -> p j t", j=J))
            if k == 0:
                nc.sync.dma_start(offsets[:], offs)
                nc.sync.dma_start(bias[:], b.rearrange("(p t) e -> p (t e)", t=G))
        wraw = [[keep.tile([P, J, N], F32, name=f"wraw{e}{a}") for a in range(PASSES)] for e in range(E)]
        wpraw = [keep.tile([P, J, M // 2], F32, name=f"wpraw{h}") for h in range(2)]
        gates = [keep.tile([P, C], F32, name=f"gates{e}") for e in range(E)]

        def load_w(e, a):
            nc.sync.dma_start(wraw[e][a][:], w[e, a * KP : (a + 1) * KP, :].rearrange("(p j) n -> p j n", j=J))

        def load_wp(h):
            nc.sync.dma_start(wpraw[h][:], wp[:, h * 256 : (h + 1) * 256].rearrange("(p j) f -> p j f", j=J))

        def load_gates(e):
            nc.sync.dma_start(gates[e][:], gate[0:P, e * C : (e + 1) * C])

        load_w(0, 0)
        load_w(0, 1)
        load_wp(0)
        load_w(1, 0)
        load_gates(0)
        load_w(1, 1)
        load_wp(1)
        load_gates(1)

        warm = keep.tile([P, 8], F32, name="warm")
        warmed = keep.tile([P, 8], F32, name="warmed")
        nc.vector.memset(warm[:], 0.0)
        nc.scalar.activation(warmed[:], warm[:], RELU)

        xbytes = keep.tile([P, T], U8, name="xbytes", align_bytes=64)
        nc.vector.memset(xbytes[:].bitcast(I32), 0)
        outt = [keep.tile([P, T], F32, name=f"outt{g}", align_bytes=64) for g in range(G)]
        for g in range(G):
            nc.gpsimd.memset(outt[g][:], 0.0)

        xgrouped = [keep.tile([P, T, J], BF16, name=f"xgrouped{a}", align_bytes=64) for a in range(PASSES)]
        xcodes = [keep.tile([P, T], U32, name=f"xcodes{a}", align_bytes=64) for a in range(PASSES)]
        gcodes = [keep.tile([P, S], U32, name=f"gcodes{a}", align_bytes=64) for a in range(PASSES)]
        gbytes = [keep.tile([P, C], U8, name="gbytes0", align_bytes=64)]
        wgrouped = [
            [
                keep.tile([P, G, P, J], BF16, name=f"wgrouped{e}{a}", tag=f"wgrouped{e}{a}", align_bytes=64)
                for a in range(PASSES)
            ]
            for e in range(E)
        ]
        wcodes = [[keep.tile([P, N], U32, name=f"wcodes{e}{a}", align_bytes=64) for a in range(PASSES)] for e in range(E)]
        wbytes = [[keep.tile([P, N], U8, name=f"wbytes{e}{a}", align_bytes=64) for a in range(PASSES)] for e in range(E)]
        wpgrouped = keep.tile([P, M, J], BF16, name="wpgrouped", align_bytes=64)
        wpcodes = keep.tile([P, M], U32, name="wpcodes", align_bytes=64)
        wpbytes = keep.tile([P, M], U8, name="wpbytes", align_bytes=64)
        y = [keep.tile([P, G, C], F32, name=f"y{e}", tag=f"y{e}", align_bytes=64) for e in range(E)]
        c = [keep.tile([P, C, J], BF16, name=f"c{e}", align_bytes=64) for e in range(E)]
        ccodes = keep.tile([P, S], U32, name="ccodes", align_bytes=64)
        cbytes = keep.tile([P, S], U8, name="cbytes", align_bytes=64)
        ybank = [psum.tile([P, C], F32, name=f"ybank{t}") for t in range(G)]
        obank = [psum.tile([P, S], F32, name=f"obank{g}") for g in range(G)]

        def move(engine, dst, src):
            if engine == "v":
                nc.vector.tensor_copy(out=dst, in_=src)
            elif engine == "s":
                nc.scalar.copy(out=dst, in_=src)
            else:
                nc.gpsimd.tensor_scalar(dst, src, 1.0, 0.0, MULT, ADD)

        def group_x(engine, a, t0, lo, hi):
            move(
                engine,
                xgrouped[a][:, t0 + lo : t0 + hi, :].rearrange("p (c i) j -> p c j i", i=4),
                xraw[a, t0][:, :, lo:hi].rearrange("p j (c i) -> p c j i", i=4),
            )

        def group_w(engine, e, a, lo, hi):
            order = "p m t j" if engine == "g" else "p m j t"
            move(
                engine,
                wgrouped[e][a][:, lo:hi, :, :].rearrange("p t m j -> " + order),
                wraw[e][a][:].rearrange("p j (m t) -> " + order, t=G)[:, :, lo:hi, :]
                if engine == "g"
                else wraw[e][a][:].rearrange("p j (m t) -> " + order, t=G)[:, :, :, lo:hi],
            )

        def group_wp(engine, h, lo, hi):
            move(
                engine,
                wpgrouped[:, h * 256 + lo : h * 256 + hi, :].rearrange("p (c i) j -> p c j i", i=4),
                wpraw[h][:, :, lo:hi].rearrange("p j (c i) -> p c j i", i=4),
            )

        def quantize_x(a, t0, t1):
            nc.vector.quantize_mx(
                out=xcodes[a][:, t0:t1].bitcast(FP8X4),
                scales=xbytes[4 * a :, t0:t1],
                in_=xgrouped[a][:, t0:t1, :].rearrange("p t j -> p (t j)"),
            )

        def quantize_w(e, a, t0, t1):
            nc.vector.quantize_mx(
                out=wcodes[e][a][:, t0 * P : t1 * P].bitcast(FP8X4),
                scales=wbytes[e][a][:, t0 * P : t1 * P],
                in_=wgrouped[e][a][:, t0:t1, :, :].rearrange("p t m j -> p (t m j)"),
            )

        def quantize_wp(f0, f1):
            nc.vector.quantize_mx(
                out=wpcodes[:, f0:f1].bitcast(FP8X4),
                scales=wpbytes[:, f0:f1],
                in_=wpgrouped[:, f0:f1, :].rearrange("p f j -> p (f j)"),
            )

        def gather_words(a, s0, s1):
            nc.vector.tensor_copy(gcodes[a][:, s0:s1], xcodes[a][:].indirect(offsets[:, s0 // 16 : s1 // 16]))

        def gather_bytes(e):
            nc.vector.tensor_copy(gbytes[e][:], xbytes[:].indirect(offsets[:, e * 16 : (e + 1) * 16]))

        def multiply(e, a, t):
            nc.tensor.matmul_mx(
                out=ybank[t][:],
                lhsT=wcodes[e][a][:, t * P : (t + 1) * P].bitcast(FP8X4),
                lhsT_scale=wbytes[e][a][:, t * P : (t + 1) * P],
                rhs=gcodes[a][:, e * C : (e + 1) * C].bitcast(FP8X4),
                rhs_scale=gbytes[e][4 * a :, :],
                start=(a == 0),
                stop=(a == PASSES - 1),
            )

        def relu(e, t):
            nc.scalar.activation(y[e][:, t, :], ybank[t][:], RELU, bias=bias[:, t * E + e : t * E + e + 1])

        def apply_gate(engine, e):
            engine.tensor_tensor(
                out=c[e][:],
                in0=y[e][:].rearrange("p t s -> p s t"),
                in1=gates[e][:].unsqueeze(2).to_broadcast([P, C, J]),
                op=MULT,
            )

        def quantize_c(e):
            nc.vector.quantize_mx(
                out=ccodes[:, e * C : (e + 1) * C].bitcast(FP8X4),
                scales=cbytes[:, e * C : (e + 1) * C],
                in_=c[e][:].rearrange("p s j -> p (s j)"),
            )

        def project(g, s0, s1):
            nc.tensor.matmul_mx(
                out=obank[g][:, s0:s1],
                lhsT=wpcodes[:, g * P : (g + 1) * P].bitcast(FP8X4),
                lhsT_scale=wpbytes[:, g * P : (g + 1) * P],
                rhs=ccodes[:, s0:s1].bitcast(FP8X4),
                rhs_scale=cbytes[:, s0:s1],
                start=True,
                stop=True,
            )
            nc.scalar.copy(out=oslots[g][:, s0:s1], in_=obank[g][:, s0:s1])

        def scatter(g, s0, s1):
            nc.vector.tensor_copy(outt[g][:].indirect(offsets[:, s0 // 16 : s1 // 16]), oslots[g][:, s0:s1])

        for a, t0, t1, cut in x_chunks:
            group_x("v", a, t0, 0, cut)
            group_x("s", a, t0, cut, t1 - t0)
            quantize_x(a, t0, t1)
            if t1 == T:
                gather_words(a, 0, S)
        group_w("g", 0, 0, 0, 2)
        group_w("s", 0, 0, 2, 4)
        quantize_w(0, 0, 0, 4)
        gather_bytes(0)
        for t in range(G):
            multiply(0, 0, t)
        for t in (0, 2):
            group_w("s", 0, 1, t, t + 1)
            group_w("v", 0, 1, t + 1, t + 2)
            quantize_w(0, 1, t, t + 2)
            for u in (t, t + 1):
                multiply(0, 1, u)
                relu(0, u)
        apply_gate(nc.vector, 0)
        quantize_c(0)
        for h, cut in ((0, 32), (1, 64)):
            group_wp("v", h, 0, cut)
            group_wp("s", h, cut, 256)
            quantize_wp(h * 256, h * 256 + 256)
        gbytes.append(keep.tile([P, C], U8, name="gbytes1", tag="wgrouped01", align_bytes=64))
        gather_bytes(1)
        for a in range(PASSES):
            group_w("s", 1, a, 0, 2)
            group_w("v", 1, a, 2, 4)
            quantize_w(1, a, 0, 4)
            for t in range(G):
                multiply(1, a, t)
                if a == PASSES - 1:
                    relu(1, t)
        late = keep.tile([P, G - 1, S], F32, name="late", tag="wgrouped11", align_bytes=64)
        oslots = [late[:, g, :] for g in range(G - 1)]
        for g in range(G - 1):
            project(g, 0, C)
            scatter(g, 0, C)
        apply_gate(nc.gpsimd, 1)
        quantize_c(1)
        last = keep.tile([P, S], F32, name="last", tag="y1", align_bytes=64)
        oslots.append(last[:])
        project(3, 0, C)
        scatter(3, 0, C)
        for g in range(G):
            project(g, C, S)
        for g in range(G):
            scatter(g, C, S)
            nc.sync.dma_start(out[g * P : (g + 1) * P, :], outt[g][:])
